import numpy as np
import ml_dtypes


def mxq(x, axis, fmt="e4m3"):
    dtype, down = {"e4m3": (ml_dtypes.float8_e4m3fn, 7), "e5m2": (ml_dtypes.float8_e5m2, 14)}[fmt]
    v = np.moveaxis(np.asarray(x, np.float32).astype(ml_dtypes.bfloat16).astype(np.float64), axis, -1)
    blocks = v.reshape(v.shape[:-1] + (-1, 32))
    amax = np.abs(blocks).max(-1, keepdims=True)
    byte = np.maximum(np.where(amax > 0, np.frexp(amax)[1] - 1 + 127, 0) - down, 1)
    scale = np.exp2(byte - 127.0)
    codes = (blocks / scale).astype(np.float32).astype(dtype).astype(np.float64)
    return np.moveaxis((codes * scale).reshape(v.shape), -1, axis)


WIDE = False


def mx_kscale(k):
    if not WIDE:
        return np.ones(k)
    levels = np.array([10, -10, 5, -5, 0])
    if k % 512:
        return np.exp2(np.random.permutation(np.resize(levels, k // 32))).repeat(32)
    a = np.empty((k // 512, 16))
    for p in range(k // 512):
        a[p, :8] = np.random.permutation(np.resize(levels, 8))
        for g in range(8):
            far = levels[np.abs(levels - a[p, g]) >= 10]
            a[p, g + 8] = far[np.random.randint(len(far))]
    return np.exp2(a.ravel()).repeat(32)


BF16 = ml_dtypes.bfloat16


def bf(x):
    return np.asarray(x, np.float32).astype(BF16)


def f64(x):
    return np.asarray(x).astype(np.float64)

def planes(Y):
    n, m = Y.shape
    b = f64(bf(Y)).reshape(n // 32, 32, m)
    amax = np.abs(b).max(1)
    byte = np.clip(np.where(amax > 0, np.frexp(amax)[1] - 1 + 127 - 7, 1), 1, 254)
    codes = (b * np.exp2(127.0 - byte)[:, None, :]).reshape(n, m).astype(np.float32).astype(ml_dtypes.float8_e4m3fn).view(np.uint8)
    words = codes.reshape(n // 512, 128, 4, m).transpose(0, 1, 3, 2)
    return np.ascontiguousarray(words), np.ascontiguousarray(byte.astype(np.uint8).reshape(n // 512, 16, m))


B, D, C, J = 1024, 1024, 1024, 1024


def softplus(v):
    return np.maximum(v, 0.0) + np.log(1.0 + np.exp(-np.abs(v)))


def sigmoid(v):
    return 1.0 / (1.0 + np.exp(-v))


def soft_hinge_gate(s, y):
    return y * sigmoid(1.0 - y * s)


def setup_inputs():
    a, u, r = mx_kscale(D), mx_kscale(C), mx_kscale(B)
    return {
        "x": bf(np.random.standard_normal((B, D)) * a),
        "w": bf(np.random.standard_normal((D, J)) * (1.5 / np.sqrt(D)) / a[:, None]),
        "c": bf(np.random.standard_normal((B, C)) * u),
        "wp": bf(np.random.standard_normal((C, J)) / np.sqrt(C) / u[:, None]),
        "lab": bf(np.random.standard_normal(B)),
        "m": bf((1.0 + 0.1 * np.random.standard_normal(B)) * r),
        "xtr": bf(np.random.standard_normal((B, D)) / r[:, None]),
    }


def core(x, w, c, wp, lab, m, xtr):
    n_batch = x.shape[0]
    n_units = w.shape[1]
    z = mxq(f64(x), 1, "e4m3") @ mxq(f64(w), 0, "e4m3")
    p = mxq(f64(c), 1, "e4m3") @ mxq(f64(wp), 0, "e4m3")
    s = np.sum(softplus(z) * p, axis=1) / np.sqrt(n_units)
    y = np.where(f64(lab) > 0, 1.0, -1.0)
    gam = soft_hinge_gate(s, y)
    post = gam[:, None] * sigmoid(z) * p * f64(m)[:, None]
    return (mxq(f64(xtr), 0, "e4m3").T @ mxq(post, 0, "e4m3")) / np.sqrt(n_batch)


def reference(x, w, c, wp, lab, m, xtr):
    R_out = core(x, w, c, wp, lab, m, xtr)
    words, scales = planes(R_out.T)
    return R_out, words, scales

@@ -1,0 +1,448 @@
+from contextlib import ExitStack
+
+import concourse.mybir as mybir
+from concourse.masks import make_identity
+
+F32 = mybir.dt.float32
+BF16 = mybir.dt.bfloat16
+U32 = mybir.dt.uint32
+I32 = mybir.dt.int32
+U8 = mybir.dt.uint8
+FP8X4 = mybir.dt.float8_e4m3fn_x4
+ACT = mybir.ActivationFunctionType
+ALU = mybir.AluOpType
+
+P = 128
+N = 1024
+FLOPS = 3 * 2 * N * N * N
+LN_FLOOR = 2.0 ** -60
+
+X0 = "vvsv"
+W0 = [128,128]
+W1 = [320,512]
+X1 = "svsv"
+C0 = "vsss"
+P0 = [512,512]
+P1 = [384,512]
+C1 = "svvs"
+GP = "gggggggvgggggggg"
+XT = "svgssgss"
+RV = "svvssvss"
+PV = "vsssssss"
+XU = [6,4,6,10,13,3,16,16]
+XQ = [10,10,16,16]
+RB = "vvvvvvvvvvvvvvvv"
+PM = "vvvv"
+
+
+def tile_clappsofthingethreefactorupdatepretrace_x1_kernel(
+    tc, x, w, c, wp, lab, m, xtr, out_0, out_1, out_2
+):
+    nc = tc.nc
+    with ExitStack() as ctx:
+        keep = ctx.enter_context(tc.tile_pool(name="keep", bufs=1))
+        raws = ctx.enter_context(tc.tile_pool(name="raws", bufs=6))
+        lay = ctx.enter_context(tc.tile_pool(name="lay", bufs=4))
+        layx = ctx.enter_context(tc.tile_pool(name="layx", bufs=3))
+        lns = ctx.enter_context(tc.tile_pool(name="lns", bufs=6))
+        outs = ctx.enter_context(tc.tile_pool(name="outs", bufs=4))
+        ps_t = ctx.enter_context(tc.psum_pool(name="ps_t", bufs=2))
+        ps_z = ctx.enter_context(tc.psum_pool(name="ps_z", bufs=3))
+        ps_p = ctx.enter_context(tc.psum_pool(name="ps_p", bufs=3))
+        ctx.enter_context(tc.manual_schedule())
+
+        ident = keep.tile([P, P], F32, name="ident")
+        warm = keep.tile([P, 1], F32, name="warm")
+        make_identity(nc, ident[:])
+        nc.scalar.activation(out=warm[:], in_=ident[:, 0:1], func=ACT.Sigmoid)
+
+        def load_cols(src, h):
+            raw = raws.tile([P, 2, 4, 512], BF16, name="raw")
+            for g in range(2):
+                nc.sync.dma_start(
+                    out=raw[:, g, :, :],
+                    in_=src[512 * g : 512 * g + 512, 512 * h : 512 * h + 512].rearrange(
+                        "(p t) j -> p t j", t=4
+                    ),
+                )
+            return raw
+
+        def load_rows(src, g, parts=1):
+            raw = raws.tile([P, 4, N], BF16, name="raw")
+            view = src[512 * g : 512 * g + 512, :].rearrange("(p t) k -> p t k", t=4)
+            n = 4 // parts
+            for k in range(parts):
+                nc.sync.dma_start(out=raw[:, n * k : n * k + n, :], in_=view[:, n * k : n * k + n, :])
+            return raw
+
+        w_raw = [None, None]
+        x_raw = [None, None]
+        wp_raw = [None, None]
+        c_raw = [None, None]
+        x_raw[0] = load_rows(x, 0, 2)
+        w_raw[0] = load_cols(w, 0)
+        w_raw[1] = load_cols(w, 1)
+        x_raw[1] = load_rows(x, 1)
+        c_raw[0] = load_rows(c, 0)
+        wp_raw[0] = load_cols(wp, 0)
+        wp_raw[1] = load_cols(wp, 1)
+        c_raw[1] = load_rows(c, 1)
+        xtr_raw = [load_rows(xtr, 0), load_rows(xtr, 1)]
+        lab_t = keep.tile([P, 2, 4], BF16, name="lab_t")
+        m_t = keep.tile([P, 2, 4], BF16, name="m_t")
+        nc.sync.dma_start(out=lab_t[:], in_=lab.rearrange("(g p t) -> p g t", g=2, t=4))
+        nc.sync.dma_start(out=m_t[:], in_=m.rearrange("(g p t) -> p g t", g=2, t=4))
+
+        def codes(nm):
+            q = keep.tile([P, 2, N], U32, name=nm + "_q", align_bytes=64)
+            s = keep.tile([P, 2, N], U8, name=nm + "_s", align_bytes=64)
+            return q, s
+
+        xq = codes("x")
+        wq = codes("w")
+        cq = codes("c")
+        wpq = codes("wp")
+        tq = codes("xtr")
+        oq = codes("post")
+        pq = codes("pout")
+
+        def quantize(dst, g, c0, width, src):
+            nc.vector.quantize_mx(
+                out=dst[0][:, g, c0 : c0 + width].bitcast(FP8X4),
+                scales=dst[1][:, g, c0 : c0 + width],
+                in_=src,
+            )
+
+        def mm(out, a, acols, b, bcols):
+            for g in range(2):
+                nc.tensor.matmul_mx(
+                    out=out,
+                    lhsT=a[0][:, g, acols].bitcast(FP8X4),
+                    lhsT_scale=a[1][:, g, acols],
+                    rhs=b[0][:, g, bcols].bitcast(FP8X4),
+                    rhs_scale=b[1][:, g, bcols],
+                    start=(g == 0),
+                    stop=(g == 1),
+                )
+
+        def flat(t):
+            return t[:].rearrange("p j t -> p (j t)")
+
+        def sl(a, n):
+            return slice(a, a + n)
+
+        def copy(eng, out, in_):
+            if eng == "v":
+                nc.vector.tensor_copy(out=out, in_=in_)
+            elif eng == "s":
+                nc.scalar.copy(out=out, in_=in_)
+            else:
+                nc.gpsimd.tensor_scalar(out=out, in0=in_, scalar1=1.0, scalar2=1.0, op0=ALU.mult, op1=ALU.mult)
+
+        def interleave_cols(raw, g, cut):
+            t = lay.tile([P, 512, 4], BF16, name="lay4", align_bytes=64)
+            src = raw[:, g, :, :].rearrange("p t j -> p j t")
+            if cut > 0:
+                copy("v", t[:, 0:cut, :], src[:, 0:cut, :])
+            if cut < 512:
+                copy("s", t[:, cut:512, :], src[:, cut:512, :])
+            return t
+
+        def turn_rows(raw, t):
+            if t % 2 == 0:
+                bank = ps_t.tile([P, 2, 2, P], F32, name="tbank")
+            else:
+                bank = ps_p.tile([P, 2, 2, P], F32, name="pbank")
+            words = raw[:].rearrange("p t k -> p (t k)").bitcast(F32)
+            for g in range(2):
+                for u in range(2):
+                    o = 512 * t + 256 * g
+                    nc.tensor.transpose(bank[:, g, u, :], words[:, o + u : o + 256 : 2], ident[:])
+            return bank
+
+        def empty_rows(eng, bank, lx, t):
+            dst = lx[:].rearrange("p g c i -> p g (c i)").bitcast(F32)[:, :, 256 * t : 256 * t + 256]
+            dst = dst.rearrange("p g (r u) -> p g r u", u=2)
+            copy(eng, dst, bank[:].rearrange("p g u r -> p g r u"))
+
+        def rows_q(dst, b, lx):
+            for g in range(2):
+                quantize(dst, g, 512 * b, 512, lx[:, g, :, :].rearrange("p c i -> p (c i)"))
+
+        gate = [keep.tile([P, 4, N], F32, name="gate0"), keep.tile([P, 4, N], F32, name="gate1")]
+
+        def zmm(i, h):
+            bank = ps_z.tile([P, 512], F32, name="zbank")
+            mm(bank[:], xq, sl(128 * i, 128), wq, sl(512 * h, 512))
+            return bank
+
+        def pmm(i, h):
+            bank = ps_p.tile([P, 512], F32, name="pbank")
+            mm(bank[:], cq, sl(128 * i, 128), wpq, sl(512 * h, 512))
+            return bank
+
+        def gview(i, h):
+            return gate[i // 4][:, i % 4, 512 * h : 512 * h + 512]
+
+        def z_sig(i, h):
+            bank = zmm(i, h)
+            nc.scalar.activation(out=gview(i, h), in_=bank[:], func=ACT.Sigmoid)
+
+        def weight_half(raw, dst, h, cuts):
+            a = interleave_cols(raw, 0, cuts[0])
+            b = interleave_cols(raw, 1, cuts[1])
+            quantize(dst, 0, 512 * h, 512, flat(a))
+            quantize(dst, 1, 512 * h, 512, flat(b))
+
+        def row_block(raw, dst, b, engs, q=True):
+            lx = layx.tile([P, 2, 512, 4], BF16, name="lx", align_bytes=64)
+            for t in range(4):
+                bank = turn_rows(raw, t)
+                empty_rows(engs[t], bank, lx, t)
+            if q:
+                rows_q(dst, b, lx)
+            return lx
+
+        row_block(x_raw[0], xq, 0, X0)
+        weight_half(w_raw[0], wq, 0, W0)
+        w1a = interleave_cols(w_raw[1], 0, W1[0])
+        w1b = interleave_cols(w_raw[1], 1, W1[1])
+        for i in range(4):
+            z_sig(i, 0)
+        quantize(wq, 0, 512, 512, flat(w1a))
+        quantize(wq, 1, 512, 512, flat(w1b))
+        row_block(x_raw[1], xq, 1, X1)
+        for i in range(4):
+            z_sig(i, 1)
+        weight_half(wp_raw[0], wpq, 0, P0)
+        for i in range(4, 6):
+            z_sig(i, 0)
+        row_block(c_raw[0], cq, 0, C0)
+        for i in range(6, 8):
+            z_sig(i, 0)
+        weight_half(wp_raw[1], wpq, 1, P1)
+        for i in range(4, 6):
+            z_sig(i, 1)
+        row_block(c_raw[1], cq, 1, C1)
+        for i in range(6, 8):
+            z_sig(i, 1)
+
+        neg_y = keep.tile([P, 8], F32, name="neg_y")
+        ym = keep.tile([P, 8], F32, name="ym")
+        pos = keep.tile([P, 8], F32, name="pos")
+        labf = lab_t[:].rearrange("p g t -> p (g t)")
+        mf = m_t[:].rearrange("p g t -> p (g t)")
+
+        sacc = keep.tile([P, 8, 2], F32, name="sacc")
+        logs = [None] * 8
+
+        def ln_tile(i):
+            logs[i] = lns.tile([P, N], F32, name="lnt")
+            nc.scalar.activation(
+                out=logs[i][:], in_=gate[i // 4][:, i % 4, :], func=ACT.Ln, bias=LN_FLOOR
+            )
+
+        for i in range(3):
+            ln_tile(i)
+
+        units = [(i, h) for i in range(8) for h in range(2)]
+        pending = [None] * 16
+        pcopy = [None] * 16
+
+        def front(u):
+            i, h = units[u]
+            if h == 0 and i >= 3:
+                ln_tile(i)
+            zb = zmm(i, h)
+            sp = logs[i][:, 512 * h : 512 * h + 512]
+            nc.vector.tensor_tensor(out=sp, in0=zb[:], in1=sp, op=ALU.subtract)
+            pending[u] = pmm(i, h)
+            if GP[u] == "g":
+                pcopy[u] = outs.tile([P, 512], F32, name="rt", bufs=8)
+                nc.scalar.copy(out=pcopy[u][:], in_=pending[u][:])
+
+        def back(u):
+            i, h = units[u]
+            sp = logs[i][:, 512 * h : 512 * h + 512]
+            pb = pending[u]
+            g = gview(i, h)
+            if GP[u] == "g":
+                nc.gpsimd.tensor_tensor(out=g, in0=pcopy[u][:], in1=g, op=ALU.mult)
+            else:
+                nc.vector.tensor_tensor(out=g, in0=pb[:], in1=g, op=ALU.mult)
+            nc.vector.scalar_tensor_tensor(
+                out=sp, in0=sp, scalar=0.0, in1=pb[:], op0=ALU.max, op1=ALU.mult,
+                accum_out=sacc[:, i, h : h + 1],
+            )
+
+        txl = [layx.tile([P, N, 4], BF16, name="lx", align_bytes=64) for k in range(2)]
+
+        def xtr_piece(k):
+            b, d = k % 2, 256 * (k // 2)
+            copy(XT[k], txl[b][:, d : d + 256, :], xtr_raw[b][:, :, d : d + 256].rearrange("p t d -> p d t"))
+
+        def xtr_q(k):
+            for b in range(2):
+                quantize(tq, b, 256 * k, 256, flat(txl[b])[:, 1024 * k : 1024 * k + 1024])
+
+        def small(k):
+            if k == 0:
+                nc.vector.tensor_scalar(out=pos[:], in0=labf, scalar1=0.0, scalar2=2.0, op0=ALU.is_gt, op1=ALU.mult)
+            if k == 1:
+                nc.vector.tensor_scalar(out=neg_y[:], in0=pos[:], scalar1=-1.0 / 32, scalar2=1.0 / 32, op0=ALU.mult, op1=ALU.add)
+            if k == 2:
+                nc.vector.scalar_tensor_tensor(out=ym[:], in0=pos[:], scalar=-1.0, in1=mf, op0=ALU.add, op1=ALU.mult)
+
+        front(0)
+        for u in range(16):
+            if u + 1 < 16:
+                front(u + 1)
+            small(u - 2)
+            for k in range(8):
+                if XU[k] == u:
+                    xtr_piece(k)
+            back(u)
+            for k in range(4):
+                if XQ[k] == u:
+                    xtr_q(k)
+
+        srow = keep.tile([P, 8], F32, name="srow")
+        gam = keep.tile([P, 8], F32, name="gam")
+        nc.vector.tensor_tensor(out=srow[:], in0=sacc[:, :, 0], in1=sacc[:, :, 1], op=ALU.add)
+        nc.vector.tensor_tensor(out=srow[:], in0=srow[:], in1=neg_y[:], op=ALU.mult)
+        nc.scalar.activation(out=gam[:], in_=srow[:], func=ACT.Sigmoid, bias=1.0)
+        nc.vector.tensor_tensor(out=gam[:], in0=gam[:], in1=ym[:], op=ALU.mult)
+
+        post = {}
+
+        def post_tile(b, h):
+            post[b, h] = lay.tile([P, 512, 4], BF16, name="lay4", align_bytes=64)
+
+        def post_tt(b, h, c0, n):
+            nc.vector.tensor_tensor(
+                out=post[b, h][:, c0 : c0 + n, :],
+                in0=gate[b][:, :, 512 * h + c0 : 512 * h + c0 + n].rearrange("p t j -> p j t"),
+                in1=gam[:, 4 * b : 4 * b + 4].unsqueeze(1).to_broadcast([P, n, 4]),
+                op=ALU.mult,
+            )
+
+        def post_scale(b, h):
+            t4 = lay.tile([P, 4, 512], BF16, name="lay4", align_bytes=64)
+            for t in range(4):
+                nc.scalar.activation(
+                    out=t4[:, t, :], in_=gate[b][:, t, 512 * h : 512 * h + 512],
+                    func=ACT.Copy, scale=gam[:, 4 * b + t : 4 * b + t + 1],
+                )
+            return t4
+
+        def post_lay(b, h, t4):
+            copy("v", post[b, h][:], t4[:].rearrange("p t j -> p j t"))
+
+        def post_q(b, h):
+            quantize(oq, b, 512 * h, 512, flat(post[b, h]))
+
+        rbank, rts, rbs, tbs, lps = {}, {}, {}, {}, {}
+
+        def rmm(r):
+            h, d = r // 8, r % 8
+            nm = "zbank" if r % 2 == 0 else "pbank"
+            pool = ps_z if r % 2 == 0 else ps_p
+            rbank[r] = pool.tile([P, 512], F32, name=nm)
+            mm(rbank[r][:], tq, sl(128 * d, 128), oq, sl(512 * h, 512))
+
+        def rev(r, eng):
+            h, d = r // 8, r % 8
+            rts[r] = outs.tile([P, 512], F32, name="rt", bufs=8)
+            if eng == "s":
+                nc.scalar.activation(out=rts[r][:], in_=rbank[r][:], func=ACT.Copy, scale=1.0 / 32)
+            else:
+                nc.vector.tensor_scalar(out=rts[r][:], in0=rbank[r][:], scalar1=1.0 / 32, scalar2=None, op0=ALU.mult)
+            nc.sync.dma_start(out=out_0[128 * d : 128 * d + 128, 512 * h : 512 * h + 512], in_=rts[r][:])
+
+        def rbf(r):
+            rbs[r] = outs.tile([P, 512], BF16, name="rb", bufs=8)
+            if RB[r] == "v":
+                nc.vector.tensor_copy(out=rbs[r][:], in_=rts[r][:])
+            else:
+                nc.gpsimd.tensor_scalar(out=rbs[r][:], in0=rts[r][:], scalar1=1.0, scalar2=1.0, op0=ALU.mult, op1=ALU.mult)
+
+        def pturn(k):
+            tbs[k] = ps_t.tile([P, 2, 2, P], F32, name="tbank")
+            for e in range(2):
+                words = rbs[2 * k + e][:].bitcast(F32)
+                for u in range(2):
+                    nc.tensor.transpose(tbs[k][:, e, u, :], words[:, u : 256 : 2], ident[:])
+
+        def pev(k, eng):
+            if k % 2 == 0:
+                lps[k // 2] = layx.tile([P, 512, 4], BF16, name="lx", align_bytes=64)
+            dst = flat(lps[k // 2]).bitcast(F32)[:, 512 * (k % 2) : 512 * (k % 2) + 512]
+            dst = dst.rearrange("p (d r u) -> p d r u", d=2, u=2)
+            copy(eng, dst, tbs[k][:].rearrange("p d u r -> p d r u"))
+
+        def pfin(k):
+            h, dh = k // 2, k % 2
+            quantize(pq, h, 512 * dh, 512, flat(lps[k]))
+            nc.sync.dma_start(
+                out=out_1[h].rearrange("p d t -> p (d t)").bitcast(I32)[:, 512 * dh : 512 * dh + 512],
+                in_=pq[0][:, h, 512 * dh : 512 * dh + 512].bitcast(I32),
+            )
+
+        def pscale(h):
+            for q in range(4):
+                nc.sync.dma_start(
+                    out=out_2[h, 4 * q : 4 * q + 4, :].bitcast(I32),
+                    in_=pq[1][32 * q : 32 * q + 4, h, :].bitcast(I32),
+                )
+
+        for h in range(2):
+            for b in range(2):
+                post_tile(b, h)
+        for k in range(8):
+            if XU[k] == 16:
+                xtr_piece(k)
+        for b, h in ((0, 0), (1, 0)):
+            if PM[2 * h + b] == "s":
+                t4 = post_scale(b, h)
+                post_lay(b, h, t4)
+            else:
+                post_tt(b, h, 0, 512)
+        post_q(0, 0)
+        post_q(1, 0)
+        for k in range(4):
+            if XQ[k] == 16:
+                xtr_q(k)
+        for r in range(6):
+            rmm(r)
+        for r in range(8):
+            rev(r, "s")
+            if r < 2:
+                rmm(r + 6)
+        for b, h in ((0, 1), (1, 1)):
+            if PM[2 * h + b] == "s":
+                t4 = post_scale(b, h)
+                post_lay(b, h, t4)
+            else:
+                post_tt(b, h, 0, 512)
+        post_q(0, 1)
+        post_q(1, 1)
+        rbf(0)
+        rbf(1)
+        for k in range(8):
+            if k < 4:
+                rmm(2 * k + 8)
+                rmm(2 * k + 9)
+            pturn(k)
+            if k < 7:
+                rbf(2 * k + 2)
+                rbf(2 * k + 3)
+            if k < 4:
+                rev(2 * k + 8, RV[2 * k])
+                rev(2 * k + 9, RV[2 * k + 1])
+            pev(k, PV[k])
+            if k % 2 == 0 and k >= 2:
+                pfin(k // 2 - 1)
+            if k == 4:
+                pscale(0)
+        pfin(3)
+        pscale(1)

@@ -18,21 +18,21 @@ FLOPS = 3 * 2 * N * N * N
 LN_FLOOR = 2.0 ** -60
 
 X0 = "vvsv"
-W0 = [128,128]
-W1 = [320,512]
-X1 = "svsv"
-C0 = "vsss"
-P0 = [512,512]
-P1 = [384,512]
-C1 = "svvs"
-GP = "gggggggvgggggggg"
-XT = "svgssgss"
-RV = "svvssvss"
-PV = "vsssssss"
-XU = [6,4,6,10,13,3,16,16]
-XQ = [10,10,16,16]
+W0 = [128,256]
+W1 = [384,320]
+X1 = "ssvs"
+C0 = "vvss"
+P0 = [384,512]
+P1 = [384,320]
+C1 = "vvvs"
+GP = "ggvggggvgggggggg"
+XT = "svssssvs"
+RV = "vssssvss"
+PV = "vsssssvs"
+XU = [5,3,3,8,14,12,7,9]
+XQ = [8,10,15,10]
 RB = "vvvvvvvvvvvvvvvv"
-PM = "vvvv"
+PM = "vssv"
 
 
 def tile_clappsofthingethreefactorupdatepretrace_x1_kernel(
@@ -139,13 +139,16 @@ def tile_clappsofthingethreefactorupdatepretrace_x1_kernel(
             else:
                 nc.gpsimd.tensor_scalar(out=out, in0=in_, scalar1=1.0, scalar2=1.0, op0=ALU.mult, op1=ALU.mult)
 
+        def by4(v):
+            return v.rearrange("p (c i) t -> p c t i", i=4)
+
         def interleave_cols(raw, g, cut):
             t = lay.tile([P, 512, 4], BF16, name="lay4", align_bytes=64)
             src = raw[:, g, :, :].rearrange("p t j -> p j t")
             if cut > 0:
-                copy("v", t[:, 0:cut, :], src[:, 0:cut, :])
+                copy("v", by4(t[:, 0:cut, :]), by4(src[:, 0:cut, :]))
             if cut < 512:
-                copy("s", t[:, cut:512, :], src[:, cut:512, :])
+                copy("s", by4(t[:, cut:512, :]), by4(src[:, cut:512, :]))
             return t
 
         def turn_rows(raw, t):
@@ -279,7 +282,7 @@ def tile_clappsofthingethreefactorupdatepretrace_x1_kernel(
 
         def xtr_piece(k):
             b, d = k % 2, 256 * (k // 2)
-            copy(XT[k], txl[b][:, d : d + 256, :], xtr_raw[b][:, :, d : d + 256].rearrange("p t d -> p d t"))
+            copy(XT[k], by4(txl[b][:, d : d + 256, :]), by4(xtr_raw[b][:, :, d : d + 256].rearrange("p t d -> p d t")))
 
         def xtr_q(k):
             for b in range(2):
@@ -320,23 +323,21 @@ def tile_clappsofthingethreefactorupdatepretrace_x1_kernel(
 
         def post_tt(b, h, c0, n):
             nc.vector.tensor_tensor(
-                out=post[b, h][:, c0 : c0 + n, :],
-                in0=gate[b][:, :, 512 * h + c0 : 512 * h + c0 + n].rearrange("p t j -> p j t"),
-                in1=gam[:, 4 * b : 4 * b + 4].unsqueeze(1).to_broadcast([P, n, 4]),
+                out=by4(post[b, h][:, c0 : c0 + n, :]),
+                in0=by4(gate[b][:, :, 512 * h + c0 : 512 * h + c0 + n].rearrange("p t j -> p j t")),
+                in1=gam[:, 4 * b : 4 * b + 4].unsqueeze(1).unsqueeze(3).to_broadcast([P, n // 4, 4, 4]),
                 op=ALU.mult,
             )
 
-        def post_scale(b, h):
-            t4 = lay.tile([P, 4, 512], BF16, name="lay4", align_bytes=64)
+        def post_scale(b, h, t4):
             for t in range(4):
                 nc.scalar.activation(
                     out=t4[:, t, :], in_=gate[b][:, t, 512 * h : 512 * h + 512],
                     func=ACT.Copy, scale=gam[:, 4 * b + t : 4 * b + t + 1],
                 )
-            return t4
 
         def post_lay(b, h, t4):
-            copy("v", post[b, h][:], t4[:].rearrange("p t j -> p j t"))
+            copy("v", by4(post[b, h][:]), by4(t4.rearrange("p t j -> p j t")))
 
         def post_q(b, h):
             quantize(oq, b, 512 * h, 512, flat(post[b, h]))
@@ -361,17 +362,17 @@ def tile_clappsofthingethreefactorupdatepretrace_x1_kernel(
 
         def rbf(r):
             rbs[r] = outs.tile([P, 512], BF16, name="rb", bufs=8)
-            if RB[r] == "v":
-                nc.vector.tensor_copy(out=rbs[r][:], in_=rts[r][:])
-            else:
-                nc.gpsimd.tensor_scalar(out=rbs[r][:], in0=rts[r][:], scalar1=1.0, scalar2=1.0, op0=ALU.mult, op1=ALU.mult)
+            nc.vector.tensor_copy(
+                out=rbs[r][:].rearrange("p (u k e) -> p u k e", u=2, e=2),
+                in_=rts[r][:].rearrange("p (k u e) -> p u k e", u=2, e=2),
+            )
 
         def pturn(k):
             tbs[k] = ps_t.tile([P, 2, 2, P], F32, name="tbank")
             for e in range(2):
                 words = rbs[2 * k + e][:].bitcast(F32)
                 for u in range(2):
-                    nc.tensor.transpose(tbs[k][:, e, u, :], words[:, u : 256 : 2], ident[:])
+                    nc.tensor.transpose(tbs[k][:, e, u, :], words[:, 128 * u : 128 * u + 128], ident[:])
 
         def pev(k, eng):
             if k % 2 == 0:
@@ -398,13 +399,18 @@ def tile_clappsofthingethreefactorupdatepretrace_x1_kernel(
         for h in range(2):
             for b in range(2):
                 post_tile(b, h)
+        t8 = layx.tile([P, 2, 4, 512], BF16, name="lx", align_bytes=64)
+        scaled = {}
+        for b, h in ((1, 0), (0, 1)):
+            if PM[2 * h + b] == "s":
+                scaled[b, h] = t8[:, h, :, :]
+                post_scale(b, h, scaled[b, h])
         for k in range(8):
             if XU[k] == 16:
                 xtr_piece(k)
         for b, h in ((0, 0), (1, 0)):
             if PM[2 * h + b] == "s":
-                t4 = post_scale(b, h)
-                post_lay(b, h, t4)
+                post_lay(b, h, scaled[b, h])
             else:
                 post_tt(b, h, 0, 512)
         post_q(0, 0)
@@ -420,8 +426,7 @@ def tile_clappsofthingethreefactorupdatepretrace_x1_kernel(
                 rmm(r + 6)
         for b, h in ((0, 1), (1, 1)):
             if PM[2 * h + b] == "s":
-                t4 = post_scale(b, h)
-                post_lay(b, h, t4)
+                post_lay(b, h, scaled[b, h])
             else:
                 post_tt(b, h, 0, 512)
         post_q(0, 1)

@@ -19,20 +19,35 @@ LN_FLOOR = 2.0 ** -60
 
 X0 = "vvsv"
 W0 = [128,256]
-W1 = [384,320]
-X1 = "ssvs"
-C0 = "vvss"
-P0 = [384,512]
-P1 = [384,320]
-C1 = "vvvs"
-GP = "ggvggggvgggggggg"
-XT = "svssssvs"
-RV = "vssssvss"
-PV = "vsssssvs"
-XU = [5,3,3,8,14,12,7,9]
-XQ = [8,10,15,10]
-RB = "vvvvvvvvvvvvvvvv"
-PM = "vssv"
+W1 = [448,512]
+X1 = "sssv"
+C0 = "vvsv"
+P0 = [512,384]
+P1 = [0,0]
+C1 = "ssvv"
+GP = "gvvvvgggvvgvvggv"
+XT = "ssgsgsss"
+RV = "svsvsvsv"
+PV = "ssssssss"
+XU = [9,10,1,11,3,12,13,14]
+XQ = [12,13,16,16]
+RB = "vvvvvvvv"
+PM = "rrrr"
+XS = 4
+SC = ["vvss","ssss","gggg","ssss"]
+EV = [0,0,4,7]
+LN0 = 2
+RBI = [7]
+LNA = 2
+AH = 5
+LR = 1
+LT = 4
+LE = 9
+SX = "vvvvvvvvvvvvvvvv"
+SL = 3
+FA = 3
+FB = 3
+RF = 0
 
 
 def tile_clappsofthingethreefactorupdatepretrace_x1_kernel(
@@ -49,328 +64,413 @@ def tile_clappsofthingethreefactorupdatepretrace_x1_kernel(
         ps_t = ctx.enter_context(tc.psum_pool(name="ps_t", bufs=2))
         ps_z = ctx.enter_context(tc.psum_pool(name="ps_z", bufs=3))
         ps_p = ctx.enter_context(tc.psum_pool(name="ps_p", bufs=3))
-        ctx.enter_context(tc.manual_schedule())
 
         ident = keep.tile([P, P], F32, name="ident")
         warm = keep.tile([P, 1], F32, name="warm")
         make_identity(nc, ident[:])
         nc.scalar.activation(out=warm[:], in_=ident[:, 0:1], func=ACT.Sigmoid)
 
-        def load_cols(src, h):
-            raw = raws.tile([P, 2, 4, 512], BF16, name="raw")
-            for g in range(2):
-                nc.sync.dma_start(
-                    out=raw[:, g, :, :],
-                    in_=src[512 * g : 512 * g + 512, 512 * h : 512 * h + 512].rearrange(
-                        "(p t) j -> p t j", t=4
-                    ),
-                )
-            return raw
+        with tc.manual_schedule():
+            def load_cols(src, h):
+                raw = raws.tile([P, 2, 4, 512], BF16, name="raw")
+                for g in range(2):
+                    nc.sync.dma_start(
+                        out=raw[:, g, :, :],
+                        in_=src[512 * g : 512 * g + 512, 512 * h : 512 * h + 512].rearrange(
+                            "(p t) j -> p t j", t=4
+                        ),
+                    )
+                return raw
 
-        def load_rows(src, g, parts=1):
-            raw = raws.tile([P, 4, N], BF16, name="raw")
-            view = src[512 * g : 512 * g + 512, :].rearrange("(p t) k -> p t k", t=4)
-            n = 4 // parts
-            for k in range(parts):
-                nc.sync.dma_start(out=raw[:, n * k : n * k + n, :], in_=view[:, n * k : n * k + n, :])
-            return raw
+            def load_rows(src, g, parts=1):
+                raw = raws.tile([P, 4, N], BF16, name="raw")
+                view = src[512 * g : 512 * g + 512, :].rearrange("(p t) k -> p t k", t=4)
+                n = 4 // parts
+                for k in range(parts):
+                    nc.sync.dma_start(out=raw[:, n * k : n * k + n, :], in_=view[:, n * k : n * k + n, :])
+                return raw
 
-        w_raw = [None, None]
-        x_raw = [None, None]
-        wp_raw = [None, None]
-        c_raw = [None, None]
-        x_raw[0] = load_rows(x, 0, 2)
-        w_raw[0] = load_cols(w, 0)
-        w_raw[1] = load_cols(w, 1)
-        x_raw[1] = load_rows(x, 1)
-        c_raw[0] = load_rows(c, 0)
-        wp_raw[0] = load_cols(wp, 0)
-        wp_raw[1] = load_cols(wp, 1)
-        c_raw[1] = load_rows(c, 1)
-        xtr_raw = [load_rows(xtr, 0), load_rows(xtr, 1)]
-        lab_t = keep.tile([P, 2, 4], BF16, name="lab_t")
-        m_t = keep.tile([P, 2, 4], BF16, name="m_t")
-        nc.sync.dma_start(out=lab_t[:], in_=lab.rearrange("(g p t) -> p g t", g=2, t=4))
-        nc.sync.dma_start(out=m_t[:], in_=m.rearrange("(g p t) -> p g t", g=2, t=4))
+            x_raw = [None, None]
+            w_raw = [None, None]
+            wp_raw = [None, None]
+            c_raw = [None, None]
+            x_raw[0] = load_rows(x, 0, 4)
+            w_raw[0] = load_cols(w, 0)
+            w_raw[1] = load_cols(w, 1)
+            x_raw[1] = load_rows(x, 1)
+            c_raw[0] = load_rows(c, 0)
+            wp_raw[0] = load_cols(wp, 0)
+            wp_raw[1] = load_cols(wp, 1)
+            c_raw[1] = load_rows(c, 1)
+            xtr_raw = [load_rows(xtr, 0), load_rows(xtr, 1)]
+            lab_t = keep.tile([P, 2, 4], BF16, name="lab_t")
+            m_t = keep.tile([P, 2, 4], BF16, name="m_t")
+            nc.sync.dma_start(out=lab_t[:], in_=lab.rearrange("(g p t) -> p g t", g=2, t=4))
+            nc.sync.dma_start(out=m_t[:], in_=m.rearrange("(g p t) -> p g t", g=2, t=4))
 
-        def codes(nm):
-            q = keep.tile([P, 2, N], U32, name=nm + "_q", align_bytes=64)
-            s = keep.tile([P, 2, N], U8, name=nm + "_s", align_bytes=64)
-            return q, s
+            def codes(nm):
+                q = keep.tile([P, 2, N], U32, name=nm + "_q", align_bytes=64)
+                s = keep.tile([P, 2, N], U8, name=nm + "_s", align_bytes=64)
+                return q, s
 
-        xq = codes("x")
-        wq = codes("w")
-        cq = codes("c")
-        wpq = codes("wp")
-        tq = codes("xtr")
-        oq = codes("post")
-        pq = codes("pout")
+            xq = codes("x")
+            wq = codes("w")
+            cq = codes("c")
+            wpq = codes("wp")
+            tq = codes("xtr")
+            oq = codes("post")
+            pq = codes("pout")
 
-        def quantize(dst, g, c0, width, src):
-            nc.vector.quantize_mx(
-                out=dst[0][:, g, c0 : c0 + width].bitcast(FP8X4),
-                scales=dst[1][:, g, c0 : c0 + width],
-                in_=src,
-            )
-
-        def mm(out, a, acols, b, bcols):
-            for g in range(2):
-                nc.tensor.matmul_mx(
-                    out=out,
-                    lhsT=a[0][:, g, acols].bitcast(FP8X4),
-                    lhsT_scale=a[1][:, g, acols],
-                    rhs=b[0][:, g, bcols].bitcast(FP8X4),
-                    rhs_scale=b[1][:, g, bcols],
-                    start=(g == 0),
-                    stop=(g == 1),
+            def quantize(dst, g, c0, width, src):
+                nc.vector.quantize_mx(
+                    out=dst[0][:, g, c0 : c0 + width].bitcast(FP8X4),
+                    scales=dst[1][:, g, c0 : c0 + width],
+                    in_=src,
                 )
 
-        def flat(t):
-            return t[:].rearrange("p j t -> p (j t)")
+            def mm(out, a, acols, b, bcols, passes=(0, 1)):
+                for g in passes:
+                    nc.tensor.matmul_mx(
+                        out=out,
+                        lhsT=a[0][:, g, acols].bitcast(FP8X4),
+                        lhsT_scale=a[1][:, g, acols],
+                        rhs=b[0][:, g, bcols].bitcast(FP8X4),
+                        rhs_scale=b[1][:, g, bcols],
+                        start=(g == 0),
+                        stop=(g == 1),
+                    )
 
-        def sl(a, n):
-            return slice(a, a + n)
+            def flat(t):
+                return t[:].rearrange("p j t -> p (j t)")
 
-        def copy(eng, out, in_):
-            if eng == "v":
-                nc.vector.tensor_copy(out=out, in_=in_)
-            elif eng == "s":
-                nc.scalar.copy(out=out, in_=in_)
-            else:
-                nc.gpsimd.tensor_scalar(out=out, in0=in_, scalar1=1.0, scalar2=1.0, op0=ALU.mult, op1=ALU.mult)
+            def sl(a, n):
+                return slice(a, a + n)
 
-        def by4(v):
-            return v.rearrange("p (c i) t -> p c t i", i=4)
+            def copy(eng, out, in_):
+                if eng == "v":
+                    nc.vector.tensor_copy(out=out, in_=in_)
+                elif eng == "s":
+                    nc.scalar.copy(out=out, in_=in_)
+                else:
+                    nc.gpsimd.tensor_scalar(out=out, in0=in_, scalar1=1.0, scalar2=1.0, op0=ALU.mult, op1=ALU.mult)
 
-        def interleave_cols(raw, g, cut):
-            t = lay.tile([P, 512, 4], BF16, name="lay4", align_bytes=64)
-            src = raw[:, g, :, :].rearrange("p t j -> p j t")
-            if cut > 0:
-                copy("v", by4(t[:, 0:cut, :]), by4(src[:, 0:cut, :]))
-            if cut < 512:
-                copy("s", by4(t[:, cut:512, :]), by4(src[:, cut:512, :]))
-            return t
+            def by4(v):
+                return v.rearrange("p (c i) t -> p c t i", i=4)
 
-        def turn_rows(raw, t):
-            if t % 2 == 0:
-                bank = ps_t.tile([P, 2, 2, P], F32, name="tbank")
-            else:
-                bank = ps_p.tile([P, 2, 2, P], F32, name="pbank")
-            words = raw[:].rearrange("p t k -> p (t k)").bitcast(F32)
-            for g in range(2):
-                for u in range(2):
-                    o = 512 * t + 256 * g
-                    nc.tensor.transpose(bank[:, g, u, :], words[:, o + u : o + 256 : 2], ident[:])
-            return bank
+            def interleave_cols(raw, g, cut):
+                t = lay.tile([P, 512, 4], BF16, name="lay4", align_bytes=64)
+                src = raw[:, g, :, :].rearrange("p t j -> p j t")
+                if cut > 0:
+                    copy("v", by4(t[:, 0:cut, :]), by4(src[:, 0:cut, :]))
+                if cut < 512:
+                    copy("s", by4(t[:, cut:512, :]), by4(src[:, cut:512, :]))
+                return t
 
-        def empty_rows(eng, bank, lx, t):
-            dst = lx[:].rearrange("p g c i -> p g (c i)").bitcast(F32)[:, :, 256 * t : 256 * t + 256]
-            dst = dst.rearrange("p g (r u) -> p g r u", u=2)
-            copy(eng, dst, bank[:].rearrange("p g u r -> p g r u"))
+            def turn_rows(raw, t):
+                if t % 2 == 0:
+                    bank = ps_t.tile([P, 2, 2, P], F32, name="tbank")
+                else:
+                    bank = ps_p.tile([P, 2, 2, P], F32, name="pbank")
+                words = raw[:].rearrange("p t k -> p (t k)").bitcast(F32)
+                for g in range(2):
+                    for u in range(2):
+                        o = 512 * t + 256 * g
+                        nc.tensor.transpose(bank[:, g, u, :], words[:, o + u : o + 256 : 2], ident[:])
+                return bank
 
-        def rows_q(dst, b, lx):
-            for g in range(2):
-                quantize(dst, g, 512 * b, 512, lx[:, g, :, :].rearrange("p c i -> p (c i)"))
+            def empty_rows(eng, bank, lx, t):
+                dst = lx[:].rearrange("p g c i -> p g (c i)").bitcast(F32)[:, :, 256 * t : 256 * t + 256]
+                dst = dst.rearrange("p g (r u) -> p g r u", u=2)
+                copy(eng, dst, bank[:].rearrange("p g u r -> p g r u"))
 
-        gate = [keep.tile([P, 4, N], F32, name="gate0"), keep.tile([P, 4, N], F32, name="gate1")]
+            def rows_q(dst, b, lx):
+                for g in range(2):
+                    quantize(dst, g, 512 * b, 512, lx[:, g, :, :].rearrange("p c i -> p (c i)"))
 
-        def zmm(i, h):
-            bank = ps_z.tile([P, 512], F32, name="zbank")
-            mm(bank[:], xq, sl(128 * i, 128), wq, sl(512 * h, 512))
-            return bank
+            gate = [keep.tile([P, 4, N], F32, name="gate0"), keep.tile([P, 4, N], F32, name="gate1")]
 
-        def pmm(i, h):
-            bank = ps_p.tile([P, 512], F32, name="pbank")
-            mm(bank[:], cq, sl(128 * i, 128), wpq, sl(512 * h, 512))
-            return bank
+            def zmm(i, h):
+                bank = ps_z.tile([P, 512], F32, name="zbank")
+                mm(bank[:], xq, sl(128 * i, 128), wq, sl(512 * h, 512))
+                return bank
 
-        def gview(i, h):
-            return gate[i // 4][:, i % 4, 512 * h : 512 * h + 512]
+            def pmm(i, h):
+                bank = ps_p.tile([P, 512], F32, name="pbank")
+                mm(bank[:], cq, sl(128 * i, 128), wpq, sl(512 * h, 512))
+                return bank
 
-        def z_sig(i, h):
-            bank = zmm(i, h)
-            nc.scalar.activation(out=gview(i, h), in_=bank[:], func=ACT.Sigmoid)
+            def gview(i, h):
+                return gate[i // 4][:, i % 4, 512 * h : 512 * h + 512]
 
-        def weight_half(raw, dst, h, cuts):
-            a = interleave_cols(raw, 0, cuts[0])
-            b = interleave_cols(raw, 1, cuts[1])
-            quantize(dst, 0, 512 * h, 512, flat(a))
-            quantize(dst, 1, 512 * h, 512, flat(b))
+            def z_sig(i, h):
+                bank = zmm(i, h)
+                nc.scalar.activation(out=gview(i, h), in_=bank[:], func=ACT.Sigmoid)
 
-        def row_block(raw, dst, b, engs, q=True):
-            lx = layx.tile([P, 2, 512, 4], BF16, name="lx", align_bytes=64)
-            for t in range(4):
-                bank = turn_rows(raw, t)
-                empty_rows(engs[t], bank, lx, t)
-            if q:
-                rows_q(dst, b, lx)
-            return lx
+            def weight_half(raw, dst, h, cuts):
+                a = interleave_cols(raw, 0, cuts[0])
+                b = interleave_cols(raw, 1, cuts[1])
+                quantize(dst, 0, 512 * h, 512, flat(a))
+                quantize(dst, 1, 512 * h, 512, flat(b))
 
-        row_block(x_raw[0], xq, 0, X0)
-        weight_half(w_raw[0], wq, 0, W0)
-        w1a = interleave_cols(w_raw[1], 0, W1[0])
-        w1b = interleave_cols(w_raw[1], 1, W1[1])
-        for i in range(4):
-            z_sig(i, 0)
-        quantize(wq, 0, 512, 512, flat(w1a))
-        quantize(wq, 1, 512, 512, flat(w1b))
-        row_block(x_raw[1], xq, 1, X1)
-        for i in range(4):
-            z_sig(i, 1)
-        weight_half(wp_raw[0], wpq, 0, P0)
-        for i in range(4, 6):
-            z_sig(i, 0)
-        row_block(c_raw[0], cq, 0, C0)
-        for i in range(6, 8):
-            z_sig(i, 0)
-        weight_half(wp_raw[1], wpq, 1, P1)
-        for i in range(4, 6):
-            z_sig(i, 1)
-        row_block(c_raw[1], cq, 1, C1)
-        for i in range(6, 8):
-            z_sig(i, 1)
+            def row_block(raw, dst, b, engs, q=True):
+                lx = layx.tile([P, 2, 512, 4], BF16, name="lx", align_bytes=64)
+                for t in range(4):
+                    bank = turn_rows(raw, t)
+                    empty_rows(engs[t], bank, lx, t)
+                if q:
+                    rows_q(dst, b, lx)
+                return lx
 
-        neg_y = keep.tile([P, 8], F32, name="neg_y")
-        ym = keep.tile([P, 8], F32, name="ym")
-        pos = keep.tile([P, 8], F32, name="pos")
-        labf = lab_t[:].rearrange("p g t -> p (g t)")
-        mf = m_t[:].rearrange("p g t -> p (g t)")
+            sacc = keep.tile([P, 8, 2], F32, name="sacc")
+            neg_y = keep.tile([P, 8], F32, name="neg_y")
+            ym = keep.tile([P, 8], F32, name="ym")
+            pos = keep.tile([P, 8], F32, name="pos")
+            labf = lab_t[:].rearrange("p g t -> p (g t)")
+            mf = m_t[:].rearrange("p g t -> p (g t)")
+            logs = {}
+            units = [(i, h) for h in range(2) for i in range(8)]
+            pending = {}
+            pcopy = {}
+            CH = [(0, 0), (1, 0), (0, 1), (1, 1)]
 
-        sacc = keep.tile([P, 8, 2], F32, name="sacc")
-        logs = [None] * 8
+            def mode(b, h):
+                return PM[CH.index((b, h))]
 
-        def ln_tile(i):
-            logs[i] = lns.tile([P, N], F32, name="lnt")
-            nc.scalar.activation(
-                out=logs[i][:], in_=gate[i // 4][:, i % 4, :], func=ACT.Ln, bias=LN_FLOOR
-            )
+            def ln_unit(u):
+                if u in logs or u > 15:
+                    return
+                logs[u] = lns.tile([P, 512], F32, name="lnt", bufs=10)
+                nc.scalar.activation(out=logs[u][:], in_=gview(*units[u]), func=ACT.Ln, bias=LN_FLOOR)
 
-        for i in range(3):
-            ln_tile(i)
+            def front(u):
+                i, h = units[u]
+                zb = zmm(i, h)
+                sp = logs[u][:]
+                nc.vector.tensor_tensor(out=sp, in0=zb[:], in1=sp, op=ALU.subtract)
+                pending[u] = pmm(i, h)
+                if (mode(i // 4, h) != "r" and GP[u] == "g") or SX[u] == "x":
+                    pc = outs.tile([P, 2, 512], F32, name="rt", bufs=4)
+                    pcopy[u] = pc[:, 0, :]
+                    nc.scalar.copy(out=pcopy[u], in_=pending[u][:])
 
-        units = [(i, h) for i in range(8) for h in range(2)]
-        pending = [None] * 16
-        pcopy = [None] * 16
+            def back(u):
+                i, h = units[u]
+                sp = logs[u][:]
+                pb = pending[u]
+                g = gview(i, h)
+                if mode(i // 4, h) != "r":
+                    if GP[u] == "g":
+                        nc.gpsimd.tensor_tensor(out=g, in0=pcopy[u], in1=g, op=ALU.mult)
+                    else:
+                        nc.vector.tensor_tensor(out=g, in0=pb[:], in1=g, op=ALU.mult)
+                if SX[u] == "x":
+                    nc.gpsimd.tensor_scalar(out=sp, in0=sp, scalar1=1e30, scalar2=0.0, op0=ALU.min, op1=ALU.max)
+                    nc.gpsimd.tensor_tensor(out=sp, in0=sp, in1=pcopy[u], op=ALU.mult)
+                    return
+                nc.vector.scalar_tensor_tensor(
+                    out=sp, in0=sp, scalar=0.0, in1=pb[:], op0=ALU.max, op1=ALU.mult,
+                    accum_out=sacc[:, i, h : h + 1],
+                )
 
-        def front(u):
-            i, h = units[u]
-            if h == 0 and i >= 3:
-                ln_tile(i)
-            zb = zmm(i, h)
-            sp = logs[i][:, 512 * h : 512 * h + 512]
-            nc.vector.tensor_tensor(out=sp, in0=zb[:], in1=sp, op=ALU.subtract)
-            pending[u] = pmm(i, h)
-            if GP[u] == "g":
-                pcopy[u] = outs.tile([P, 512], F32, name="rt", bufs=8)
-                nc.scalar.copy(out=pcopy[u][:], in_=pending[u][:])
+            def late_sum(u):
+                i, h = units[u]
+                if SX[u] == "x":
+                    nc.scalar.activation(
+                        out=logs[u][:], in_=logs[u][:], func=ACT.Copy, accum_out=sacc[:, i, h : h + 1]
+                    )
 
-        def back(u):
-            i, h = units[u]
-            sp = logs[i][:, 512 * h : 512 * h + 512]
-            pb = pending[u]
-            g = gview(i, h)
-            if GP[u] == "g":
-                nc.gpsimd.tensor_tensor(out=g, in0=pcopy[u][:], in1=g, op=ALU.mult)
-            else:
-                nc.vector.tensor_tensor(out=g, in0=pb[:], in1=g, op=ALU.mult)
-            nc.vector.scalar_tensor_tensor(
-                out=sp, in0=sp, scalar=0.0, in1=pb[:], op0=ALU.max, op1=ALU.mult,
-                accum_out=sacc[:, i, h : h + 1],
-            )
+            txl = {}
 
-        txl = [layx.tile([P, N, 4], BF16, name="lx", align_bytes=64) for k in range(2)]
+            def xtr_piece(k):
+                b, d = k % 2, 256 * (k // 2)
+                if b not in txl:
+                    txl[b] = layx.tile([P, N, 4], BF16, name="lx", align_bytes=64)
+                copy(XT[k], by4(txl[b][:, d : d + 256, :]), by4(xtr_raw[b][:, :, d : d + 256].rearrange("p t d -> p d t")))
 
-        def xtr_piece(k):
-            b, d = k % 2, 256 * (k // 2)
-            copy(XT[k], by4(txl[b][:, d : d + 256, :]), by4(xtr_raw[b][:, :, d : d + 256].rearrange("p t d -> p d t")))
+            def xtr_q(k):
+                for b in range(2):
+                    quantize(tq, b, 256 * k, 256, flat(txl[b])[:, 1024 * k : 1024 * k + 1024])
 
-        def xtr_q(k):
-            for b in range(2):
-                quantize(tq, b, 256 * k, 256, flat(txl[b])[:, 1024 * k : 1024 * k + 1024])
+            def small(k):
+                if k == 0:
+                    nc.vector.tensor_scalar(out=pos[:], in0=labf, scalar1=0.0, scalar2=2.0, op0=ALU.is_gt, op1=ALU.mult)
+                if k == 1:
+                    nc.vector.tensor_scalar(out=neg_y[:], in0=pos[:], scalar1=-1.0 / 32, scalar2=1.0 / 32, op0=ALU.mult, op1=ALU.add)
+                if k == 2:
+                    nc.vector.scalar_tensor_tensor(out=ym[:], in0=pos[:], scalar=-1.0, in1=mf, op0=ALU.add, op1=ALU.mult)
 
-        def small(k):
-            if k == 0:
-                nc.vector.tensor_scalar(out=pos[:], in0=labf, scalar1=0.0, scalar2=2.0, op0=ALU.is_gt, op1=ALU.mult)
-            if k == 1:
-                nc.vector.tensor_scalar(out=neg_y[:], in0=pos[:], scalar1=-1.0 / 32, scalar2=1.0 / 32, op0=ALU.mult, op1=ALU.add)
-            if k == 2:
-                nc.vector.scalar_tensor_tensor(out=ym[:], in0=pos[:], scalar=-1.0, in1=mf, op0=ALU.add, op1=ALU.mult)
+            row_block(x_raw[0], xq, 0, X0)
+            weight_half(w_raw[0], wq, 0, W0)
+            w1a = interleave_cols(w_raw[1], 0, W1[0])
+            w1b = interleave_cols(w_raw[1], 1, W1[1])
+            for i in range(4):
+                z_sig(i, 0)
+            quantize(wq, 0, 512, 512, flat(w1a))
+            quantize(wq, 1, 512, 512, flat(w1b))
+            row_block(x_raw[1], xq, 1, X1)
+            for i in range(4):
+                z_sig(i, 1)
+            weight_half(wp_raw[0], wpq, 0, P0)
+            for i in range(4, 6):
+                z_sig(i, 0)
+            row_block(c_raw[0], cq, 0, C0)
+            for i in range(6, 8):
+                z_sig(i, 0)
+            for i in range(4, 8):
+                z_sig(i, 1)
+            hold = {}
+            if EV[0] == 0:
+                row_block(c_raw[1], cq, 1, C1)
+            for u in range(LN0):
+                ln_unit(u)
 
-        front(0)
-        for u in range(16):
-            if u + 1 < 16:
-                front(u + 1)
-            small(u - 2)
-            for k in range(8):
-                if XU[k] == u:
-                    xtr_piece(k)
-            back(u)
-            for k in range(4):
-                if XQ[k] == u:
-                    xtr_q(k)
+            def event(u):
+                if u == EV[0]:
+                    hold["c1"] = row_block(c_raw[1], cq, 1, C1, q=False)
+                if u == EV[1]:
+                    rows_q(cq, 1, hold["c1"])
+                if u == EV[2]:
+                    hold["wp"] = [interleave_cols(wp_raw[1], g, P1[g]) for g in range(2)]
+                if u == EV[3]:
+                    for g in range(2):
+                        quantize(wpq, g, 512, 512, flat(hold["wp"][g]))
+                for k in range(8):
+                    if XU[k] == u:
+                        xtr_piece(k)
+                for k in range(4):
+                    if XQ[k] == u:
+                        xtr_q(k)
 
-        srow = keep.tile([P, 8], F32, name="srow")
-        gam = keep.tile([P, 8], F32, name="gam")
-        nc.vector.tensor_tensor(out=srow[:], in0=sacc[:, :, 0], in1=sacc[:, :, 1], op=ALU.add)
-        nc.vector.tensor_tensor(out=srow[:], in0=srow[:], in1=neg_y[:], op=ALU.mult)
-        nc.scalar.activation(out=gam[:], in_=srow[:], func=ACT.Sigmoid, bias=1.0)
-        nc.vector.tensor_tensor(out=gam[:], in0=gam[:], in1=ym[:], op=ALU.mult)
+            front(0)
+            for u in range(16):
+                if u + 1 < 16:
+                    for q in range(u + 2 + LNA):
+                        ln_unit(q)
+                    event(u + 1)
+                    front(u + 1)
+                small(u - 8)
+                back(u)
+                if u >= SL:
+                    late_sum(u - SL)
+
+            for u in range(16 - SL, 16):
+                late_sum(u)
+
+            srow = keep.tile([P, 8], F32, name="srow")
+            gam = keep.tile([P, 8], F32, name="gam")
+            nc.vector.tensor_tensor(out=srow[:], in0=sacc[:, :, 0], in1=sacc[:, :, 1], op=ALU.add)
+            gap = [k for k in range(4) if XQ[k] == 16]
+            for k in gap[:1]:
+                xtr_q(k)
+            nc.vector.tensor_tensor(out=srow[:], in0=srow[:], in1=neg_y[:], op=ALU.mult)
+            for k in gap[1:]:
+                xtr_q(k)
+            nc.scalar.activation(out=gam[:], in_=srow[:], func=ACT.Sigmoid, bias=1.0)
+            nc.vector.tensor_tensor(out=gam[:], in0=gam[:], in1=ym[:], op=ALU.mult)
 
         post = {}
+        scaled = {}
 
-        def post_tile(b, h):
+        def gate_quarter(b, h):
+            return gate[b][:, :, 512 * h : 512 * h + 512]
+
+        def prepare(b, h):
+            k = CH.index((b, h))
             post[b, h] = lay.tile([P, 512, 4], BF16, name="lay4", align_bytes=64)
-
-        def post_tt(b, h, c0, n):
-            nc.vector.tensor_tensor(
-                out=by4(post[b, h][:, c0 : c0 + n, :]),
-                in0=by4(gate[b][:, :, 512 * h + c0 : 512 * h + c0 + n].rearrange("p t j -> p j t")),
-                in1=gam[:, 4 * b : 4 * b + 4].unsqueeze(1).unsqueeze(3).to_broadcast([P, n // 4, 4, 4]),
-                op=ALU.mult,
-            )
-
-        def post_scale(b, h, t4):
+            if PM[k] == "l":
+                if "t8" not in scaled:
+                    scaled["t8"] = layx.tile([P, 2, 4, 512], BF16, name="lx", align_bytes=64)
+                dst = scaled["t8"][:, h, :, :]
+                scaled[b, h] = dst
+            else:
+                dst = gate_quarter(b, h)
+            if PM[k] == "t":
+                return
             for t in range(4):
-                nc.scalar.activation(
-                    out=t4[:, t, :], in_=gate[b][:, t, 512 * h : 512 * h + 512],
-                    func=ACT.Copy, scale=gam[:, 4 * b + t : 4 * b + t + 1],
-                )
+                src = gate[b][:, t, 512 * h : 512 * h + 512]
+                f = gam[:, 4 * b + t : 4 * b + t + 1]
+                e = SC[k][t]
+                if e == "s":
+                    nc.scalar.activation(out=dst[:, t, :], in_=src, func=ACT.Copy, scale=f)
+                elif e == "v":
+                    nc.vector.tensor_scalar(out=dst[:, t, :], in0=src, scalar1=f, scalar2=None, op0=ALU.mult)
+                else:
+                    nc.gpsimd.tensor_scalar(out=dst[:, t, :], in0=src, scalar1=f, scalar2=1.0, op0=ALU.mult, op1=ALU.mult)
 
-        def post_lay(b, h, t4):
-            copy("v", by4(post[b, h][:]), by4(t4.rearrange("p t j -> p j t")))
+        pbanks = {}
+
+        def p_again(b, h, jc):
+            if mode(b, h) != "r":
+                return
+            where = "pppzzztt"[4 * b + jc] if h == 0 else "pppttppp"[4 * b + jc]
+            pool, nm = {"p": (ps_p, "pbank"), "z": (ps_z, "zbank"), "t": (ps_t, "tbank")}[where]
+            bank = pool.tile([P, 4, P], F32, name=nm)
+            for t in range(4):
+                mm(bank[:, t, :], cq, sl(512 * b + 128 * t, 128), wpq, sl(512 * h + 128 * jc, 128))
+            pbanks[b, h, jc] = bank
+
+        def piece(b, h, jc):
+            out = by4(post[b, h][:, 128 * jc : 128 * jc + 128, :])
+            md = mode(b, h)
+            if md == "l":
+                copy("v", out, by4(scaled[b, h][:, :, 128 * jc : 128 * jc + 128].rearrange("p t j -> p j t")))
+                return
+            g = by4(gate_quarter(b, h)[:, :, 128 * jc : 128 * jc + 128].rearrange("p t j -> p j t"))
+            if md == "t":
+                in1 = gam[:, 4 * b : 4 * b + 4].unsqueeze(1).unsqueeze(3).to_broadcast([P, 32, 4, 4])
+            else:
+                in1 = by4(pbanks[b, h, jc][:].rearrange("p t j -> p j t"))
+            nc.vector.tensor_tensor(out=out, in0=g, in1=in1, op=ALU.mult)
 
         def post_q(b, h):
             quantize(oq, b, 512 * h, 512, flat(post[b, h]))
 
         rbank, rts, rbs, tbs, lps = {}, {}, {}, {}, {}
 
+        def rmm_first(r):
+            h, d = r // 8, r % 8
+            in_z = r < 8 or r % 2 == 0
+            nm = "zbank" if in_z else "pbank"
+            pool = ps_z if in_z else ps_p
+            rbank[r] = pool.tile([P, 512], F32, name=nm)
+            mm(rbank[r][:], tq, sl(128 * d, 128), oq, sl(512 * h, 512), (0,))
+
         def rmm(r):
             h, d = r // 8, r % 8
-            nm = "zbank" if r % 2 == 0 else "pbank"
-            pool = ps_z if r % 2 == 0 else ps_p
-            rbank[r] = pool.tile([P, 512], F32, name=nm)
-            mm(rbank[r][:], tq, sl(128 * d, 128), oq, sl(512 * h, 512))
+            if r not in rbank:
+                rmm_first(r)
+            mm(rbank[r][:], tq, sl(128 * d, 128), oq, sl(512 * h, 512), (1,))
 
         def rev(r, eng):
             h, d = r // 8, r % 8
-            rts[r] = outs.tile([P, 512], F32, name="rt", bufs=8)
+            if r % 2 == 0:
+                rts[r // 2] = outs.tile([P, 2, 512], F32, name="rt", bufs=4)
+            rt = rts[r // 2][:, r % 2, :]
             if eng == "s":
-                nc.scalar.activation(out=rts[r][:], in_=rbank[r][:], func=ACT.Copy, scale=1.0 / 32)
+                nc.scalar.activation(out=rt, in_=rbank[r][:], func=ACT.Copy, scale=1.0 / 32)
             else:
-                nc.vector.tensor_scalar(out=rts[r][:], in0=rbank[r][:], scalar1=1.0 / 32, scalar2=None, op0=ALU.mult)
-            nc.sync.dma_start(out=out_0[128 * d : 128 * d + 128, 512 * h : 512 * h + 512], in_=rts[r][:])
+                nc.vector.tensor_scalar(out=rt, in0=rbank[r][:], scalar1=1.0 / 32, scalar2=None, op0=ALU.mult)
+            if r % 2 == 1:
+                nc.sync.dma_start(
+                    out=out_0[128 * d - 128 : 128 * d + 128, 512 * h : 512 * h + 512].rearrange(
+                        "(e p) j -> p e j", e=2
+                    ),
+                    in_=rts[r // 2][:],
+                )
 
-        def rbf(r):
-            rbs[r] = outs.tile([P, 512], BF16, name="rb", bufs=8)
-            nc.vector.tensor_copy(
-                out=rbs[r][:].rearrange("p (u k e) -> p u k e", u=2, e=2),
-                in_=rts[r][:].rearrange("p (k u e) -> p u k e", u=2, e=2),
-            )
+        def rbf(k):
+            rbs[k] = outs.tile([P, 2, 512], BF16, name="rb", bufs=4)
+            for q in range(2):
+                copy(
+                    RB[k],
+                    rbs[k][:, q, :].rearrange("p (u k e) -> p u k e", u=2, e=2),
+                    rts[k][:, q, :].rearrange("p (k u e) -> p u k e", u=2, e=2),
+                )
 
         def pturn(k):
             tbs[k] = ps_t.tile([P, 2, 2, P], F32, name="tbank")
             for e in range(2):
-                words = rbs[2 * k + e][:].bitcast(F32)
+                words = rbs[k][:, e, :].bitcast(F32)
                 for u in range(2):
                     nc.tensor.transpose(tbs[k][:, e, u, :], words[:, 128 * u : 128 * u + 128], ident[:])
 
@@ -396,58 +496,82 @@ def tile_clappsofthingethreefactorupdatepretrace_x1_kernel(
                     in_=pq[1][32 * q : 32 * q + 4, h, :].bitcast(I32),
                 )
 
-        for h in range(2):
-            for b in range(2):
-                post_tile(b, h)
-        t8 = layx.tile([P, 2, 4, 512], BF16, name="lx", align_bytes=64)
-        scaled = {}
-        for b, h in ((1, 0), (0, 1)):
-            if PM[2 * h + b] == "s":
-                scaled[b, h] = t8[:, h, :, :]
-                post_scale(b, h, scaled[b, h])
-        for k in range(8):
-            if XU[k] == 16:
-                xtr_piece(k)
-        for b, h in ((0, 0), (1, 0)):
-            if PM[2 * h + b] == "s":
-                post_lay(b, h, scaled[b, h])
-            else:
-                post_tt(b, h, 0, 512)
-        post_q(0, 0)
+        prepare(0, 0)
+        prepare(1, 0)
+        for s in range(8):
+            p_again(s // 4, 0, s % 4)
+        for s in range(8):
+            if s == 4:
+                prepare(0, 1)
+            piece(s // 4, 0, s % 4)
+            if s < 3:
+                p_again(0, 1, s)
+            if s >= 6:
+                p_again((s - 3) // 4, 1, (s - 3) % 4)
+            if s == 5:
+                post_q(0, 0)
         post_q(1, 0)
-        for k in range(4):
-            if XQ[k] == 16:
-                xtr_q(k)
-        for r in range(6):
-            rmm(r)
-        for r in range(8):
-            rev(r, "s")
-            if r < 2:
-                rmm(r + 6)
-        for b, h in ((0, 1), (1, 1)):
-            if PM[2 * h + b] == "s":
-                post_lay(b, h, scaled[b, h])
-            else:
-                post_tt(b, h, 0, 512)
-        post_q(0, 1)
+        prepare(1, 1)
+        rmm(0)
+        rmm(1)
+        rmm(2)
+        seen = {"r": 0, "t": 0, "e": 0}
+
+        def do_rbf(n):
+            while seen["r"] < n:
+                rbf(seen["r"])
+                seen["r"] += 1
+
+        def do_turn(n):
+            while seen["t"] < n:
+                pturn(seen["t"])
+                seen["t"] += 1
+
+        def do_ev(n):
+            while seen["e"] < n:
+                k = seen["e"]
+                pev(k, PV[k])
+                seen["e"] += 1
+
+        for s in range(8):
+            b, jc = s // 4, s % 4
+            piece(b, 1, jc)
+            if s + 5 < 8:
+                p_again((s + 5) // 4, 1, (s + 5) % 4)
+            rev(s, "s")
+            if s + 3 < 8:
+                rmm(s + 3)
+            if s == 5:
+                post_q(0, 1)
+            do_rbf(max(0, (s + 1 - LR) // 2))
+            do_turn(max(0, (s + 1 - LT) // 2))
+            do_ev(max(0, (s + 1 - LE) // 2))
+            if s >= 6 and s - 6 < RF:
+                rmm_first(s + 2)
         post_q(1, 1)
-        rbf(0)
-        rbf(1)
-        for k in range(8):
-            if k < 4:
-                rmm(2 * k + 8)
-                rmm(2 * k + 9)
-            pturn(k)
-            if k < 7:
-                rbf(2 * k + 2)
-                rbf(2 * k + 3)
-            if k < 4:
-                rev(2 * k + 8, RV[2 * k])
-                rev(2 * k + 9, RV[2 * k + 1])
-            pev(k, PV[k])
-            if k % 2 == 0 and k >= 2:
-                pfin(k // 2 - 1)
-            if k == 4:
-                pscale(0)
+        for r in range(8, 14):
+            rmm(r)
+        do_rbf(4)
+        do_turn(2)
+        for k in range(4):
+            rev(2 * k + 8, RV[2 * k])
+            rev(2 * k + 9, RV[2 * k + 1])
+            if k == 0:
+                rmm(14)
+                rmm(15)
+            do_rbf(k + 5)
+            do_ev(k + 1)
+            do_turn(k + 3)
+            if k == FA:
+                pfin(0)
+            if k == FB:
+                pfin(1)
+        pscale(0)
+        do_ev(5)
+        do_turn(7)
+        do_ev(6)
+        do_turn(8)
+        pfin(2)
+        do_ev(8)
         pfin(3)
         pscale(1)

from contextlib import ExitStack

import concourse.mybir as mybir
from concourse.masks import make_identity

F32 = mybir.dt.float32
BF16 = mybir.dt.bfloat16
U32 = mybir.dt.uint32
I32 = mybir.dt.int32
U8 = mybir.dt.uint8
FP8X4 = mybir.dt.float8_e4m3fn_x4
ACT = mybir.ActivationFunctionType
ALU = mybir.AluOpType

P = 128
N = 1024
FLOPS = 3 * 2 * N * N * N
LN_FLOOR = 2.0 ** -60

X0 = "vvsv"
W0 = [128,256]
W1 = [448,512]
X1 = "sssv"
C0 = "vvsv"
P0 = [512,384]
P1 = [0,0]
C1 = "ssvv"
GP = "gvvvvgggvvgvvggv"
XT = "ssgsgsss"
RV = "svsvsvsv"
PV = "ssssssss"
XU = [9,10,1,11,3,12,13,14]
XQ = [12,13,16,16]
RB = "vvvvvvvv"
PM = "rrrr"
XS = 4
SC = ["vvss","ssss","gggg","ssss"]
EV = [0,0,4,7]
LN0 = 2
RBI = [7]
LNA = 2
AH = 5
LR = 1
LT = 4
LE = 9
SX = "vvvvvvvvvvvvvvvv"
SL = 3
FA = 3
FB = 3
RF = 0


def tile_clappsofthingethreefactorupdatepretrace_x1_kernel(
    tc, x, w, c, wp, lab, m, xtr, out_0, out_1, out_2
):
    nc = tc.nc
    with ExitStack() as ctx:
        keep = ctx.enter_context(tc.tile_pool(name="keep", bufs=1))
        raws = ctx.enter_context(tc.tile_pool(name="raws", bufs=6))
        lay = ctx.enter_context(tc.tile_pool(name="lay", bufs=4))
        layx = ctx.enter_context(tc.tile_pool(name="layx", bufs=3))
        lns = ctx.enter_context(tc.tile_pool(name="lns", bufs=6))
        outs = ctx.enter_context(tc.tile_pool(name="outs", bufs=4))
        ps_t = ctx.enter_context(tc.psum_pool(name="ps_t", bufs=2))
        ps_z = ctx.enter_context(tc.psum_pool(name="ps_z", bufs=3))
        ps_p = ctx.enter_context(tc.psum_pool(name="ps_p", bufs=3))

        ident = keep.tile([P, P], F32, name="ident")
        warm = keep.tile([P, 1], F32, name="warm")
        make_identity(nc, ident[:])
        nc.scalar.activation(out=warm[:], in_=ident[:, 0:1], func=ACT.Sigmoid)

        with tc.manual_schedule():
            def load_cols(src, h):
                raw = raws.tile([P, 2, 4, 512], BF16, name="raw")
                for g in range(2):
                    nc.sync.dma_start(
                        out=raw[:, g, :, :],
                        in_=src[512 * g : 512 * g + 512, 512 * h : 512 * h + 512].rearrange(
                            "(p t) j -> p t j", t=4
                        ),
                    )
                return raw

            def load_rows(src, g, parts=1):
                raw = raws.tile([P, 4, N], BF16, name="raw")
                view = src[512 * g : 512 * g + 512, :].rearrange("(p t) k -> p t k", t=4)
                n = 4 // parts
                for k in range(parts):
                    nc.sync.dma_start(out=raw[:, n * k : n * k + n, :], in_=view[:, n * k : n * k + n, :])
                return raw

            x_raw = [None, None]
            w_raw = [None, None]
            wp_raw = [None, None]
            c_raw = [None, None]
            x_raw[0] = load_rows(x, 0, 4)
            w_raw[0] = load_cols(w, 0)
            w_raw[1] = load_cols(w, 1)
            x_raw[1] = load_rows(x, 1)
            c_raw[0] = load_rows(c, 0)
            wp_raw[0] = load_cols(wp, 0)
            wp_raw[1] = load_cols(wp, 1)
            c_raw[1] = load_rows(c, 1)
            xtr_raw = [load_rows(xtr, 0), load_rows(xtr, 1)]
            lab_t = keep.tile([P, 2, 4], BF16, name="lab_t")
            m_t = keep.tile([P, 2, 4], BF16, name="m_t")
            nc.sync.dma_start(out=lab_t[:], in_=lab.rearrange("(g p t) -> p g t", g=2, t=4))
            nc.sync.dma_start(out=m_t[:], in_=m.rearrange("(g p t) -> p g t", g=2, t=4))

            def codes(nm):
                q = keep.tile([P, 2, N], U32, name=nm + "_q", align_bytes=64)
                s = keep.tile([P, 2, N], U8, name=nm + "_s", align_bytes=64)
                return q, s

            xq = codes("x")
            wq = codes("w")
            cq = codes("c")
            wpq = codes("wp")
            tq = codes("xtr")
            oq = codes("post")
            pq = codes("pout")

            def quantize(dst, g, c0, width, src):
                nc.vector.quantize_mx(
                    out=dst[0][:, g, c0 : c0 + width].bitcast(FP8X4),
                    scales=dst[1][:, g, c0 : c0 + width],
                    in_=src,
                )

            def mm(out, a, acols, b, bcols, passes=(0, 1)):
                for g in passes:
                    nc.tensor.matmul_mx(
                        out=out,
                        lhsT=a[0][:, g, acols].bitcast(FP8X4),
                        lhsT_scale=a[1][:, g, acols],
                        rhs=b[0][:, g, bcols].bitcast(FP8X4),
                        rhs_scale=b[1][:, g, bcols],
                        start=(g == 0),
                        stop=(g == 1),
                    )

            def flat(t):
                return t[:].rearrange("p j t -> p (j t)")

            def sl(a, n):
                return slice(a, a + n)

            def copy(eng, out, in_):
                if eng == "v":
                    nc.vector.tensor_copy(out=out, in_=in_)
                elif eng == "s":
                    nc.scalar.copy(out=out, in_=in_)
                else:
                    nc.gpsimd.tensor_scalar(out=out, in0=in_, scalar1=1.0, scalar2=1.0, op0=ALU.mult, op1=ALU.mult)

            def by4(v):
                return v.rearrange("p (c i) t -> p c t i", i=4)

            def interleave_cols(raw, g, cut):
                t = lay.tile([P, 512, 4], BF16, name="lay4", align_bytes=64)
                src = raw[:, g, :, :].rearrange("p t j -> p j t")
                if cut > 0:
                    copy("v", by4(t[:, 0:cut, :]), by4(src[:, 0:cut, :]))
                if cut < 512:
                    copy("s", by4(t[:, cut:512, :]), by4(src[:, cut:512, :]))
                return t

            def turn_rows(raw, t):
                if t % 2 == 0:
                    bank = ps_t.tile([P, 2, 2, P], F32, name="tbank")
                else:
                    bank = ps_p.tile([P, 2, 2, P], F32, name="pbank")
                words = raw[:].rearrange("p t k -> p (t k)").bitcast(F32)
                for g in range(2):
                    for u in range(2):
                        o = 512 * t + 256 * g
                        nc.tensor.transpose(bank[:, g, u, :], words[:, o + u : o + 256 : 2], ident[:])
                return bank

            def empty_rows(eng, bank, lx, t):
                dst = lx[:].rearrange("p g c i -> p g (c i)").bitcast(F32)[:, :, 256 * t : 256 * t + 256]
                dst = dst.rearrange("p g (r u) -> p g r u", u=2)
                copy(eng, dst, bank[:].rearrange("p g u r -> p g r u"))

            def rows_q(dst, b, lx):
                for g in range(2):
                    quantize(dst, g, 512 * b, 512, lx[:, g, :, :].rearrange("p c i -> p (c i)"))

            gate = [keep.tile([P, 4, N], F32, name="gate0"), keep.tile([P, 4, N], F32, name="gate1")]

            def zmm(i, h):
                bank = ps_z.tile([P, 512], F32, name="zbank")
                mm(bank[:], xq, sl(128 * i, 128), wq, sl(512 * h, 512))
                return bank

            def pmm(i, h):
                bank = ps_p.tile([P, 512], F32, name="pbank")
                mm(bank[:], cq, sl(128 * i, 128), wpq, sl(512 * h, 512))
                return bank

            def gview(i, h):
                return gate[i // 4][:, i % 4, 512 * h : 512 * h + 512]

            def z_sig(i, h):
                bank = zmm(i, h)
                nc.scalar.activation(out=gview(i, h), in_=bank[:], func=ACT.Sigmoid)

            def weight_half(raw, dst, h, cuts):
                a = interleave_cols(raw, 0, cuts[0])
                b = interleave_cols(raw, 1, cuts[1])
                quantize(dst, 0, 512 * h, 512, flat(a))
                quantize(dst, 1, 512 * h, 512, flat(b))

            def row_block(raw, dst, b, engs, q=True):
                lx = layx.tile([P, 2, 512, 4], BF16, name="lx", align_bytes=64)
                for t in range(4):
                    bank = turn_rows(raw, t)
                    empty_rows(engs[t], bank, lx, t)
                if q:
                    rows_q(dst, b, lx)
                return lx

            sacc = keep.tile([P, 8, 2], F32, name="sacc")
            neg_y = keep.tile([P, 8], F32, name="neg_y")
            ym = keep.tile([P, 8], F32, name="ym")
            pos = keep.tile([P, 8], F32, name="pos")
            labf = lab_t[:].rearrange("p g t -> p (g t)")
            mf = m_t[:].rearrange("p g t -> p (g t)")
            logs = {}
            units = [(i, h) for h in range(2) for i in range(8)]
            pending = {}
            pcopy = {}
            CH = [(0, 0), (1, 0), (0, 1), (1, 1)]

            def mode(b, h):
                return PM[CH.index((b, h))]

            def ln_unit(u):
                if u in logs or u > 15:
                    return
                logs[u] = lns.tile([P, 512], F32, name="lnt", bufs=10)
                nc.scalar.activation(out=logs[u][:], in_=gview(*units[u]), func=ACT.Ln, bias=LN_FLOOR)

            def front(u):
                i, h = units[u]
                zb = zmm(i, h)
                sp = logs[u][:]
                nc.vector.tensor_tensor(out=sp, in0=zb[:], in1=sp, op=ALU.subtract)
                pending[u] = pmm(i, h)
                if (mode(i // 4, h) != "r" and GP[u] == "g") or SX[u] == "x":
                    pc = outs.tile([P, 2, 512], F32, name="rt", bufs=4)
                    pcopy[u] = pc[:, 0, :]
                    nc.scalar.copy(out=pcopy[u], in_=pending[u][:])

            def back(u):
                i, h = units[u]
                sp = logs[u][:]
                pb = pending[u]
                g = gview(i, h)
                if mode(i // 4, h) != "r":
                    if GP[u] == "g":
                        nc.gpsimd.tensor_tensor(out=g, in0=pcopy[u], in1=g, op=ALU.mult)
                    else:
                        nc.vector.tensor_tensor(out=g, in0=pb[:], in1=g, op=ALU.mult)
                if SX[u] == "x":
                    nc.gpsimd.tensor_scalar(out=sp, in0=sp, scalar1=1e30, scalar2=0.0, op0=ALU.min, op1=ALU.max)
                    nc.gpsimd.tensor_tensor(out=sp, in0=sp, in1=pcopy[u], op=ALU.mult)
                    return
                nc.vector.scalar_tensor_tensor(
                    out=sp, in0=sp, scalar=0.0, in1=pb[:], op0=ALU.max, op1=ALU.mult,
                    accum_out=sacc[:, i, h : h + 1],
                )

            def late_sum(u):
                i, h = units[u]
                if SX[u] == "x":
                    nc.scalar.activation(
                        out=logs[u][:], in_=logs[u][:], func=ACT.Copy, accum_out=sacc[:, i, h : h + 1]
                    )

            txl = {}

            def xtr_piece(k):
                b, d = k % 2, 256 * (k // 2)
                if b not in txl:
                    txl[b] = layx.tile([P, N, 4], BF16, name="lx", align_bytes=64)
                copy(XT[k], by4(txl[b][:, d : d + 256, :]), by4(xtr_raw[b][:, :, d : d + 256].rearrange("p t d -> p d t")))

            def xtr_q(k):
                for b in range(2):
                    quantize(tq, b, 256 * k, 256, flat(txl[b])[:, 1024 * k : 1024 * k + 1024])

            def small(k):
                if k == 0:
                    nc.vector.tensor_scalar(out=pos[:], in0=labf, scalar1=0.0, scalar2=2.0, op0=ALU.is_gt, op1=ALU.mult)
                if k == 1:
                    nc.vector.tensor_scalar(out=neg_y[:], in0=pos[:], scalar1=-1.0 / 32, scalar2=1.0 / 32, op0=ALU.mult, op1=ALU.add)
                if k == 2:
                    nc.vector.scalar_tensor_tensor(out=ym[:], in0=pos[:], scalar=-1.0, in1=mf, op0=ALU.add, op1=ALU.mult)

            row_block(x_raw[0], xq, 0, X0)
            weight_half(w_raw[0], wq, 0, W0)
            w1a = interleave_cols(w_raw[1], 0, W1[0])
            w1b = interleave_cols(w_raw[1], 1, W1[1])
            for i in range(4):
                z_sig(i, 0)
            quantize(wq, 0, 512, 512, flat(w1a))
            quantize(wq, 1, 512, 512, flat(w1b))
            row_block(x_raw[1], xq, 1, X1)
            for i in range(4):
                z_sig(i, 1)
            weight_half(wp_raw[0], wpq, 0, P0)
            for i in range(4, 6):
                z_sig(i, 0)
            row_block(c_raw[0], cq, 0, C0)
            for i in range(6, 8):
                z_sig(i, 0)
            for i in range(4, 8):
                z_sig(i, 1)
            hold = {}
            if EV[0] == 0:
                row_block(c_raw[1], cq, 1, C1)
            for u in range(LN0):
                ln_unit(u)

            def event(u):
                if u == EV[0]:
                    hold["c1"] = row_block(c_raw[1], cq, 1, C1, q=False)
                if u == EV[1]:
                    rows_q(cq, 1, hold["c1"])
                if u == EV[2]:
                    hold["wp"] = [interleave_cols(wp_raw[1], g, P1[g]) for g in range(2)]
                if u == EV[3]:
                    for g in range(2):
                        quantize(wpq, g, 512, 512, flat(hold["wp"][g]))
                for k in range(8):
                    if XU[k] == u:
                        xtr_piece(k)
                for k in range(4):
                    if XQ[k] == u:
                        xtr_q(k)

            front(0)
            for u in range(16):
                if u + 1 < 16:
                    for q in range(u + 2 + LNA):
                        ln_unit(q)
                    event(u + 1)
                    front(u + 1)
                small(u - 8)
                back(u)
                if u >= SL:
                    late_sum(u - SL)

            for u in range(16 - SL, 16):
                late_sum(u)

            srow = keep.tile([P, 8], F32, name="srow")
            gam = keep.tile([P, 8], F32, name="gam")
            nc.vector.tensor_tensor(out=srow[:], in0=sacc[:, :, 0], in1=sacc[:, :, 1], op=ALU.add)
            gap = [k for k in range(4) if XQ[k] == 16]
            for k in gap[:1]:
                xtr_q(k)
            nc.vector.tensor_tensor(out=srow[:], in0=srow[:], in1=neg_y[:], op=ALU.mult)
            for k in gap[1:]:
                xtr_q(k)
            nc.scalar.activation(out=gam[:], in_=srow[:], func=ACT.Sigmoid, bias=1.0)
            nc.vector.tensor_tensor(out=gam[:], in0=gam[:], in1=ym[:], op=ALU.mult)

        post = {}
        scaled = {}

        def gate_quarter(b, h):
            return gate[b][:, :, 512 * h : 512 * h + 512]

        def prepare(b, h):
            k = CH.index((b, h))
            post[b, h] = lay.tile([P, 512, 4], BF16, name="lay4", align_bytes=64)
            if PM[k] == "l":
                if "t8" not in scaled:
                    scaled["t8"] = layx.tile([P, 2, 4, 512], BF16, name="lx", align_bytes=64)
                dst = scaled["t8"][:, h, :, :]
                scaled[b, h] = dst
            else:
                dst = gate_quarter(b, h)
            if PM[k] == "t":
                return
            for t in range(4):
                src = gate[b][:, t, 512 * h : 512 * h + 512]
                f = gam[:, 4 * b + t : 4 * b + t + 1]
                e = SC[k][t]
                if e == "s":
                    nc.scalar.activation(out=dst[:, t, :], in_=src, func=ACT.Copy, scale=f)
                elif e == "v":
                    nc.vector.tensor_scalar(out=dst[:, t, :], in0=src, scalar1=f, scalar2=None, op0=ALU.mult)
                else:
                    nc.gpsimd.tensor_scalar(out=dst[:, t, :], in0=src, scalar1=f, scalar2=1.0, op0=ALU.mult, op1=ALU.mult)

        pbanks = {}

        def p_again(b, h, jc):
            if mode(b, h) != "r":
                return
            where = "pppzzztt"[4 * b + jc] if h == 0 else "pppttppp"[4 * b + jc]
            pool, nm = {"p": (ps_p, "pbank"), "z": (ps_z, "zbank"), "t": (ps_t, "tbank")}[where]
            bank = pool.tile([P, 4, P], F32, name=nm)
            for t in range(4):
                mm(bank[:, t, :], cq, sl(512 * b + 128 * t, 128), wpq, sl(512 * h + 128 * jc, 128))
            pbanks[b, h, jc] = bank

        def piece(b, h, jc):
            out = by4(post[b, h][:, 128 * jc : 128 * jc + 128, :])
            md = mode(b, h)
            if md == "l":
                copy("v", out, by4(scaled[b, h][:, :, 128 * jc : 128 * jc + 128].rearrange("p t j -> p j t")))
                return
            g = by4(gate_quarter(b, h)[:, :, 128 * jc : 128 * jc + 128].rearrange("p t j -> p j t"))
            if md == "t":
                in1 = gam[:, 4 * b : 4 * b + 4].unsqueeze(1).unsqueeze(3).to_broadcast([P, 32, 4, 4])
            else:
                in1 = by4(pbanks[b, h, jc][:].rearrange("p t j -> p j t"))
            nc.vector.tensor_tensor(out=out, in0=g, in1=in1, op=ALU.mult)

        def post_q(b, h):
            quantize(oq, b, 512 * h, 512, flat(post[b, h]))

        rbank, rts, rbs, tbs, lps = {}, {}, {}, {}, {}

        def rmm_first(r):
            h, d = r // 8, r % 8
            in_z = r < 8 or r % 2 == 0
            nm = "zbank" if in_z else "pbank"
            pool = ps_z if in_z else ps_p
            rbank[r] = pool.tile([P, 512], F32, name=nm)
            mm(rbank[r][:], tq, sl(128 * d, 128), oq, sl(512 * h, 512), (0,))

        def rmm(r):
            h, d = r // 8, r % 8
            if r not in rbank:
                rmm_first(r)
            mm(rbank[r][:], tq, sl(128 * d, 128), oq, sl(512 * h, 512), (1,))

        def rev(r, eng):
            h, d = r // 8, r % 8
            if r % 2 == 0:
                rts[r // 2] = outs.tile([P, 2, 512], F32, name="rt", bufs=4)
            rt = rts[r // 2][:, r % 2, :]
            if eng == "s":
                nc.scalar.activation(out=rt, in_=rbank[r][:], func=ACT.Copy, scale=1.0 / 32)
            else:
                nc.vector.tensor_scalar(out=rt, in0=rbank[r][:], scalar1=1.0 / 32, scalar2=None, op0=ALU.mult)
            if r % 2 == 1:
                nc.sync.dma_start(
                    out=out_0[128 * d - 128 : 128 * d + 128, 512 * h : 512 * h + 512].rearrange(
                        "(e p) j -> p e j", e=2
                    ),
                    in_=rts[r // 2][:],
                )

        def rbf(k):
            rbs[k] = outs.tile([P, 2, 512], BF16, name="rb", bufs=4)
            for q in range(2):
                copy(
                    RB[k],
                    rbs[k][:, q, :].rearrange("p (u k e) -> p u k e", u=2, e=2),
                    rts[k][:, q, :].rearrange("p (k u e) -> p u k e", u=2, e=2),
                )

        def pturn(k):
            tbs[k] = ps_t.tile([P, 2, 2, P], F32, name="tbank")
            for e in range(2):
                words = rbs[k][:, e, :].bitcast(F32)
                for u in range(2):
                    nc.tensor.transpose(tbs[k][:, e, u, :], words[:, 128 * u : 128 * u + 128], ident[:])

        def pev(k, eng):
            if k % 2 == 0:
                lps[k // 2] = layx.tile([P, 512, 4], BF16, name="lx", align_bytes=64)
            dst = flat(lps[k // 2]).bitcast(F32)[:, 512 * (k % 2) : 512 * (k % 2) + 512]
            dst = dst.rearrange("p (d r u) -> p d r u", d=2, u=2)
            copy(eng, dst, tbs[k][:].rearrange("p d u r -> p d r u"))

        def pfin(k):
            h, dh = k // 2, k % 2
            quantize(pq, h, 512 * dh, 512, flat(lps[k]))
            nc.sync.dma_start(
                out=out_1[h].rearrange("p d t -> p (d t)").bitcast(I32)[:, 512 * dh : 512 * dh + 512],
                in_=pq[0][:, h, 512 * dh : 512 * dh + 512].bitcast(I32),
            )

        def pscale(h):
            for q in range(4):
                nc.sync.dma_start(
                    out=out_2[h, 4 * q : 4 * q + 4, :].bitcast(I32),
                    in_=pq[1][32 * q : 32 * q + 4, h, :].bitcast(I32),
                )

        prepare(0, 0)
        prepare(1, 0)
        for s in range(8):
            p_again(s // 4, 0, s % 4)
        for s in range(8):
            if s == 4:
                prepare(0, 1)
            piece(s // 4, 0, s % 4)
            if s < 3:
                p_again(0, 1, s)
            if s >= 6:
                p_again((s - 3) // 4, 1, (s - 3) % 4)
            if s == 5:
                post_q(0, 0)
        post_q(1, 0)
        prepare(1, 1)
        rmm(0)
        rmm(1)
        rmm(2)
        seen = {"r": 0, "t": 0, "e": 0}

        def do_rbf(n):
            while seen["r"] < n:
                rbf(seen["r"])
                seen["r"] += 1

        def do_turn(n):
            while seen["t"] < n:
                pturn(seen["t"])
                seen["t"] += 1

        def do_ev(n):
            while seen["e"] < n:
                k = seen["e"]
                pev(k, PV[k])
                seen["e"] += 1

        for s in range(8):
            b, jc = s // 4, s % 4
            piece(b, 1, jc)
            if s + 5 < 8:
                p_again((s + 5) // 4, 1, (s + 5) % 4)
            rev(s, "s")
            if s + 3 < 8:
                rmm(s + 3)
            if s == 5:
                post_q(0, 1)
            do_rbf(max(0, (s + 1 - LR) // 2))
            do_turn(max(0, (s + 1 - LT) // 2))
            do_ev(max(0, (s + 1 - LE) // 2))
            if s >= 6 and s - 6 < RF:
                rmm_first(s + 2)
        post_q(1, 1)
        for r in range(8, 14):
            rmm(r)
        do_rbf(4)
        do_turn(2)
        for k in range(4):
            rev(2 * k + 8, RV[2 * k])
            rev(2 * k + 9, RV[2 * k + 1])
            if k == 0:
                rmm(14)
                rmm(15)
            do_rbf(k + 5)
            do_ev(k + 1)
            do_turn(k + 3)
            if k == FA:
                pfin(0)
            if k == FB:
                pfin(1)
        pscale(0)
        do_ev(5)
        do_turn(7)
        do_ev(6)
        do_turn(8)
        pfin(2)
        do_ev(8)
        pfin(3)
        pscale(1)
